import numpy as np
import ml_dtypes


def mxq(x, axis, fmt="e4m3"):
    dtype, down = {"e4m3": (ml_dtypes.float8_e4m3fn, 7), "e5m2": (ml_dtypes.float8_e5m2, 14)}[fmt]
    v = np.moveaxis(np.asarray(x, np.float32).astype(ml_dtypes.bfloat16).astype(np.float64), axis, -1)
    blocks = v.reshape(v.shape[:-1] + (-1, 32))
    amax = np.abs(blocks).max(-1, keepdims=True)
    byte = np.maximum(np.where(amax > 0, np.frexp(amax)[1] - 1 + 127, 0) - down, 1)
    scale = np.exp2(byte - 127.0)
    codes = (blocks / scale).astype(np.float32).astype(dtype).astype(np.float64)
    return np.moveaxis((codes * scale).reshape(v.shape), -1, axis)


WIDE = False


def mx_kscale(k):
    if not WIDE:
        return np.ones(k)
    levels = np.array([10, -10, 5, -5, 0])
    if k % 512:
        return np.exp2(np.random.permutation(np.resize(levels, k // 32))).repeat(32)
    a = np.empty((k // 512, 16))
    for p in range(k // 512):
        a[p, :8] = np.random.permutation(np.resize(levels, 8))
        for g in range(8):
            far = levels[np.abs(levels - a[p, g]) >= 10]
            a[p, g + 8] = far[np.random.randint(len(far))]
    return np.exp2(a.ravel()).repeat(32)


def f64(x):
    return np.asarray(x).astype(np.float64)


def striped(idx):
    return np.tile(idx.reshape(-1, 16).T, (8, 1)).astype(np.uint16)


def unstriped(offs):
    return offs[:16].T.reshape(-1).astype(np.int64)


E2M1 = np.array([0.0, 0.5, 1.0, 1.5, 2.0, 3.0, 4.0, 6.0, -0.0, -0.5, -1.0, -1.5, -2.0, -3.0, -4.0, -6.0])


def pack_weight(w, fmt):
    k, n = w.shape
    w = f64(np.asarray(w, np.float32).astype(ml_dtypes.bfloat16)).reshape(k // 32, 32, n)
    amax = np.abs(w).max(1)
    if fmt == "e4m3":
        byte = np.frexp(amax)[1] - 1 + 127 - 7
    else:
        mant, ex = np.frexp(amax / 6.0)
        byte = np.where(mant > 0.5, ex, ex - 1) + 127
    byte = np.clip(np.where(amax > 0, byte, 1), 1, 254)
    scaled = (w * np.exp2(127.0 - byte)[:, None, :]).reshape(k, n).astype(np.float32)
    by_word = np.ascontiguousarray(scaled.reshape(k // 512, 128, 4, n).transpose(0, 1, 3, 2))
    if fmt == "e4m3":
        words = by_word.astype(ml_dtypes.float8_e4m3fn).view(np.uint8)
    else:
        c = by_word.astype(ml_dtypes.float4_e2m1fn).view(np.uint8) & 0xF
        words = (c[..., 0::2] | (c[..., 1::2] << 4)).reshape(k // 512, 128, 2 * n)
    return np.ascontiguousarray(words), np.ascontiguousarray(byte.astype(np.uint8).reshape(k // 512, 16, n))


def unpack_weight(words, scales, fmt):
    g, _, n = scales.shape
    words = np.ascontiguousarray(words).reshape(g, 128, n, -1)
    if fmt == "e4m3":
        vals = words.view(ml_dtypes.float8_e4m3fn).astype(np.float64)
    else:
        nib = np.empty((g, 128, n, 4), np.uint8)
        nib[..., 0::2] = words & 0xF
        nib[..., 1::2] = words >> 4
        vals = E2M1[nib]
    vals = vals * np.repeat(np.exp2(scales.astype(np.float64) - 127.0), 8, axis=1)[..., None]
    return vals.transpose(0, 1, 3, 2).reshape(g * 512, n)


def gelu(v):
    return 0.5 * v * (1.0 + np.tanh(np.sqrt(2.0 / np.pi) * (v + 0.044715 * v**3)))


K, T, S, H, T2, P = 1536, 2048, 1024, 512, 2048, 512


def setup_inputs():
    n = np.random.standard_normal
    s = mx_kscale(K)[:, None]
    u = mx_kscale(H)[:, None]
    tab_words, tab_scales = pack_weight(n((K, T)) * s, "e4m3")
    w1 = 1.6 * n((K, H)) / np.sqrt(K) / s
    w2_words, w2_scales = pack_weight(n((H, H)) / np.sqrt(H) / u, "e2m1")
    perm = np.random.permutation(T2)
    return {
        "tab_words": tab_words, "tab_scales": tab_scales,
        "offs": striped(np.random.permutation(T)[:S]),
        "w1": w1.astype(np.float32),
        "page0": n((H, T2)).astype(np.float32),
        "wgs": np.exp(0.3 * n((128, S))).astype(np.float32),
        "offs2": striped(np.random.permutation(T2)[:S]),
        "offs3": striped(perm[:P]),
        "offs4": striped(perm[P:2 * P]),
        "va": (0.8 * n(H)).astype(np.float32),
        "vb": (0.8 * n(H)).astype(np.float32),
        "gain": (np.exp(0.3 * n(H)) * u[:, 0]).astype(np.float32),
        "w2_words": w2_words, "w2_scales": w2_scales,
    }


def reference(tab_words, tab_scales, offs, w1, page0, wgs, offs2, offs3, offs4, va, vb, gain, w2_words, w2_scales):
    v = unpack_weight(tab_words, tab_scales, "e4m3")[:, unstriped(offs)]
    h = np.tanh(mxq(f64(w1), 0, "e4m3").T @ v)
    page = f64(page0).copy()
    page[:, unstriped(offs2)] = np.tile(f64(wgs), (H // 128, 1)) * h
    a = page[:, unstriped(offs3)]
    b = page[:, unstriped(offs4)]
    page[:, unstriped(offs3)] = f64(va)[:, None] * a + b
    page[:, unstriped(offs4)] = f64(vb)[:, None] * b + a
    x = mxq(f64(gain)[:, None] * page, 0, "e4m3")
    w2 = unpack_weight(w2_words, w2_scales, "e2m1")
    return (w2.T @ x) + page

@@ -1,0 +1,275 @@
+from contextlib import ExitStack
+
+import concourse.mybir as mybir
+
+K, T, S, H, T2, PAIRS = 1536, 2048, 1024, 512, 2048, 512
+FLOPS = 2 * K * H * S + 2 * H * H * T2
+
+F32 = mybir.dt.float32
+BF16 = mybir.dt.bfloat16
+I32 = mybir.dt.int32
+U32 = mybir.dt.uint32
+U16 = mybir.dt.uint16
+U8 = mybir.dt.uint8
+FP8X4 = mybir.dt.float8_e4m3fn_x4
+FP4X4 = mybir.dt.float4_e2m1fn_x4
+MULT = mybir.AluOpType.mult
+ADD = mybir.AluOpType.add
+COPY = mybir.ActivationFunctionType.Copy
+TANH = mybir.ActivationFunctionType.Tanh
+
+P = 128
+PACK = 4
+PASSES = K // (P * PACK)
+HALF = S // 2
+FIRST_PAIR = (0, 2)
+SECOND_PAIR = (1, 3)
+CHUNKS = (256, 256, 512, 512, 512)
+
+
+def tile_list_duty_swap_board_kernel(
+    tc, tab_words, tab_scales, offs, w1, page0, wgs, offs2, offs3, offs4, va, vb, gain, w2_words, w2_scales, out
+):
+    nc = tc.nc
+    with ExitStack() as ctx:
+        lists = ctx.enter_context(tc.tile_pool(name="lists", bufs=1))
+        keep = ctx.enter_context(tc.tile_pool(name="keep", bufs=1))
+        swap = ctx.enter_context(tc.tile_pool(name="swap", bufs=2))
+        psum = ctx.enter_context(tc.psum_pool(name="psum", bufs=8))
+
+        l1 = lists.tile([P, S // 16], U16, name="l1")
+        l2 = lists.tile([P, S // 16], U16, name="l2")
+        l3 = lists.tile([P, PAIRS // 16], U16, name="l3")
+        l4 = lists.tile([P, PAIRS // 16], U16, name="l4")
+
+        words = [keep.tile([P, T], U32, name="words%d" % a, align_bytes=64) for a in range(PASSES)]
+        planes = keep.tile([P, T], U8, name="planes", align_bytes=64)
+        w1_raw = [keep.tile([P, PACK, H], F32, name="w1_raw%d" % a) for a in range(PASSES)]
+        page = [keep.tile([P, T2], F32, name="page%d" % t, align_bytes=64) for t in range(PACK)]
+        wg = [keep.tile([P, S], F32, name="wg%d" % t) for t in range(PACK)]
+        w2_raw = keep.tile([P, 2 * H], U8, name="w2_raw", align_bytes=64)
+        w2s_raw = keep.tile([P, H], U8, name="w2s_raw", align_bytes=64)
+        va_t = keep.tile([P, PACK], F32, name="va_t")
+        vb_t = keep.tile([P, PACK], F32, name="vb_t")
+        gain_t = keep.tile([P, PACK], F32, name="gain_t")
+
+        nc.vector.memset(planes[:].bitcast(I32), 0)
+        nc.gpsimd.memset(w2s_raw[:].bitcast(I32), 0)
+
+        page_rows = page0.rearrange("(p t) c -> t p c", t=PACK)
+        wgs_rows = wgs.rearrange("(q t) s -> t q s", t=PACK)
+
+        def load_words(a):
+            nc.sync.dma_start(
+                out=words[a][:].bitcast(I32), in_=tab_words[a].rearrange("p n i -> p (n i)").bitcast(I32)
+            )
+
+        def load_w1(a):
+            nc.sync.dma_start(
+                out=w1_raw[a][:], in_=w1[512 * a : 512 * (a + 1), :].rearrange("(p j) c -> p j c", j=PACK)
+            )
+
+        def load_wg(t, c0, c1):
+            for quad in (0, 2, 1, 3):
+                nc.sync.dma_start(out=wg[t][32 * quad : 32 * quad + 32, c0:c1], in_=wgs_rows[t][:, c0:c1])
+
+        first = FIRST_PAIR[0]
+        nc.sync.dma_start(l1[:], offs)
+        load_words(0)
+        for quad in range(4):
+            nc.scalar.dma_start(
+                out=planes[32 * quad : 32 * quad + 4 * PASSES, :].bitcast(I32),
+                in_=tab_scales[:, 4 * quad : 4 * quad + 4, :].bitcast(I32),
+            )
+        load_w1(0)
+        nc.sync.dma_start(out=w2_raw[:].bitcast(I32), in_=w2_words[0].bitcast(I32))
+        for quad in range(4):
+            nc.scalar.dma_start(
+                out=w2s_raw[32 * quad : 32 * quad + 4, :].bitcast(I32),
+                in_=w2_scales[0, 4 * quad : 4 * quad + 4, :].bitcast(I32),
+            )
+        load_w1(1)
+        load_words(1)
+        load_w1(2)
+        load_words(2)
+        nc.sync.dma_start(l2[:], offs2)
+        load_wg(first, 0, HALF)
+        nc.sync.dma_start(out=page[first][:], in_=page_rows[first])
+        load_wg(first, HALF, S)
+        nc.sync.dma_start(out=page[FIRST_PAIR[1]][:], in_=page_rows[FIRST_PAIR[1]])
+        load_wg(FIRST_PAIR[1], 0, S)
+        nc.sync.dma_start(l3[:], offs3)
+        nc.sync.dma_start(l4[:], offs4)
+        nc.sync.dma_start(out=va_t[:], in_=va.rearrange("(p t) -> p t", t=PACK))
+        nc.sync.dma_start(out=vb_t[:], in_=vb.rearrange("(p t) -> p t", t=PACK))
+        nc.sync.dma_start(out=gain_t[:], in_=gain.rearrange("(p t) -> p t", t=PACK))
+        for t in SECOND_PAIR:
+            nc.sync.dma_start(out=page[t][:], in_=page_rows[t])
+        for t in reversed(SECOND_PAIR):
+            load_wg(t, 0, S)
+
+        picked = [keep.tile([P, S], U32, name="picked%d" % a, align_bytes=64) for a in range(PASSES)]
+        picked_planes = keep.tile([P, S], U8, name="picked_planes", align_bytes=64)
+        w1_bf = [keep.tile([P, PACK, P, PACK], BF16, name="w1_bf%d" % a, align_bytes=64) for a in range(PASSES)]
+        w1_codes = [keep.tile([P, H], U32, name="w1_codes%d" % a, align_bytes=64) for a in range(PASSES)]
+        w1_scales = [keep.tile([P, H], U8, name="w1_scales%d" % a, align_bytes=64) for a in range(PASSES)]
+        w2_codes = keep.tile([P, 2 * H], U8, name="w2_codes", align_bytes=64)
+        w2_planes = keep.tile([P, H], U8, name="w2_planes", align_bytes=64)
+
+        def weave_w1(a):
+            dst = w1_bf[a][:].rearrange("p t m j -> p m t j")
+            src = w1_raw[a][:].rearrange("p j (m t) -> p m t j", t=PACK)
+            if a < PASSES - 1:
+                nc.scalar.copy(out=dst, in_=src)
+            else:
+                nc.vector.tensor_copy(out=dst, in_=src)
+
+        def quantize_w1(a):
+            nc.vector.quantize_mx(
+                out=w1_codes[a][:].bitcast(FP8X4),
+                scales=w1_scales[a][:],
+                in_=w1_bf[a][:].rearrange("p t m j -> p (t m j)"),
+            )
+
+        nc.vector.tensor_copy(picked[0][:], words[0][:].indirect(l1[:]))
+        nc.vector.tensor_copy(picked_planes[:], planes[:].indirect(l1[:]))
+        weave_w1(0)
+        nc.vector.tensor_copy(
+            out=w2_codes[:].rearrange("p (t m b) -> p t m b", t=PACK, b=2),
+            in_=w2_raw[:].rearrange("p (m t b) -> p t m b", t=PACK, b=2),
+        )
+        nc.vector.tensor_copy(
+            out=w2_planes[:].rearrange("p (t m) -> p t m", t=PACK),
+            in_=w2s_raw[:].rearrange("p (m t) -> p t m", t=PACK),
+        )
+        quantize_w1(0)
+        weave_w1(1)
+        nc.vector.tensor_copy(picked[1][:], words[1][:].indirect(l1[:]))
+        quantize_w1(1)
+        weave_w1(2)
+        quantize_w1(2)
+        for half in range(2):
+            nc.vector.tensor_copy(
+                picked[2][:, half * HALF : (half + 1) * HALF],
+                words[2][:].indirect(l1[:, half * (HALF // 16) : (half + 1) * (HALF // 16)]),
+            )
+
+        h = [keep.tile([P, S], F32, name="h%d" % t) for t in range(PACK)]
+        groups = [(t, half) for t in FIRST_PAIR + SECOND_PAIR for half in range(2)]
+        sums = {g: psum.tile([P, HALF], F32, name="bank") for g in groups}
+        for a in range(PASSES):
+            for t, half in groups:
+                cols = slice(half * HALF, (half + 1) * HALF)
+                nc.tensor.matmul_mx(
+                    out=sums[t, half][:],
+                    lhsT=w1_codes[a][:, t * P : (t + 1) * P].bitcast(FP8X4),
+                    lhsT_scale=w1_scales[a][:, t * P : (t + 1) * P],
+                    rhs=picked[a][:, cols].bitcast(FP8X4),
+                    rhs_scale=picked_planes[4 * a : P, cols],
+                    start=(a == 0),
+                    stop=(a == PASSES - 1),
+                )
+        for t, half in groups:
+            nc.scalar.activation(out=h[t][:, half * HALF : (half + 1) * HALF], in_=sums[t, half][:], func=TANH)
+
+        starts = [sum(CHUNKS[:c]) for c in range(len(CHUNKS))]
+        x_bf = [keep.tile([P, w, PACK], BF16, name="x_bf%d" % c, align_bytes=64) for c, w in enumerate(CHUNKS)]
+
+        def put(t):
+            if t == first:
+                for half in range(2):
+                    cols = slice(half * HALF, (half + 1) * HALF)
+                    nc.vector.tensor_tensor(
+                        page[t][:].indirect(l2[:, half * (HALF // 16) : (half + 1) * (HALF // 16)]),
+                        h[t][:, cols],
+                        wg[t][:, cols],
+                        MULT,
+                    )
+            else:
+                nc.vector.tensor_tensor(page[t][:].indirect(l2[:]), h[t][:], wg[t][:], MULT)
+
+        def fetch(t, offsets, factor, tag):
+            side = swap.tile([P, PAIRS], F32, name="side_" + tag)
+            scaled = swap.tile([P, PAIRS], F32, name="scaled_" + tag)
+            nc.vector.tensor_copy(side[:], page[t][:].indirect(offsets[:]))
+            nc.scalar.activation(out=scaled[:], in_=side[:], func=COPY, scale=factor[:, t : t + 1])
+            return side, scaled
+
+        def put_back(t, offsets, scaled, other):
+            nc.vector.tensor_tensor(page[t][:].indirect(offsets[:]), scaled[:], other[:], ADD)
+
+        def round_rows(t, c):
+            cols = slice(starts[c], starts[c] + CHUNKS[c])
+            nc.scalar.activation(out=x_bf[c][:, :, t], in_=page[t][:, cols], func=COPY, scale=gain_t[:, t : t + 1])
+
+        t0, t1 = FIRST_PAIR
+        put(t0)
+        put(t1)
+        a0, va0 = fetch(t0, l3, va_t, "a")
+        a1, va1 = fetch(t1, l3, va_t, "a")
+        b0, vb0 = fetch(t0, l4, vb_t, "b")
+        b1, vb1 = fetch(t1, l4, vb_t, "b")
+        put_back(t0, l3, va0, b0)
+        put_back(t1, l3, va1, b1)
+        put_back(t0, l4, vb0, a0)
+        put_back(t1, l4, vb1, a1)
+        for t in FIRST_PAIR:
+            for c in range(len(CHUNKS)):
+                round_rows(t, c)
+
+        t0, t1 = SECOND_PAIR
+        put(t0)
+        put(t1)
+        a0, va0 = fetch(t0, l3, va_t, "a")
+        b0, vb0 = fetch(t0, l4, vb_t, "b")
+        a1, va1 = fetch(t1, l3, va_t, "a")
+        put_back(t0, l3, va0, b0)
+        b1, vb1 = fetch(t1, l4, vb_t, "b")
+        put_back(t0, l4, vb0, a0)
+        put_back(t1, l3, va1, b1)
+        put_back(t1, l4, vb1, a1)
+        for c in range(len(CHUNKS)):
+            round_rows(t0, c)
+
+        out_rows = out.rearrange("(p t) c -> p t c", t=PACK)
+        x_codes = [keep.tile([P, w], U32, name="x_codes%d" % c, align_bytes=64) for c, w in enumerate(CHUNKS)]
+        x_scales = [keep.tile([P, w], U8, name="x_scales%d" % c, align_bytes=64) for c, w in enumerate(CHUNKS)]
+        result = [keep.tile([P, PACK, w], F32, name="result%d" % c) for c, w in enumerate(CHUNKS)]
+
+        def quantize_x(c):
+            nc.vector.quantize_mx(
+                out=x_codes[c][:].bitcast(FP8X4), scales=x_scales[c][:], in_=x_bf[c][:].rearrange("p w i -> p (w i)")
+            )
+
+        def finish(c):
+            w = CHUNKS[c]
+            cols = slice(starts[c], starts[c] + w)
+            for t in range(PACK):
+                acc = psum.tile([P, HALF], F32, name="bank")
+                nc.tensor.matmul_mx(
+                    out=acc[:, 0:w],
+                    lhsT=w2_codes[:, 2 * t * P : 2 * (t + 1) * P].bitcast(FP4X4),
+                    lhsT_scale=w2_planes[:, t * P : (t + 1) * P],
+                    rhs=x_codes[c][:].bitcast(FP8X4),
+                    rhs_scale=x_scales[c][:],
+                    start=True,
+                    stop=True,
+                )
+                nc.vector.tensor_tensor(result[c][:, t, :], acc[:, 0:w], page[t][:, cols], ADD)
+                if t % 2 == 1:
+                    nc.sync.dma_start(out=out_rows[:, t - 1 : t + 1, cols], in_=result[c][:, t - 1 : t + 1, :])
+
+        nc.vector.tensor_scalar(
+            out=x_bf[0][:, :, t1],
+            in0=page[t1][:, 0 : CHUNKS[0]],
+            scalar1=gain_t[:, t1 : t1 + 1],
+            scalar2=None,
+            op0=MULT,
+        )
+        for c in range(1, len(CHUNKS)):
+            round_rows(t1, c)
+        quantize_x(0)
+        for c in range(len(CHUNKS)):
+            if c + 1 < len(CHUNKS):
+                quantize_x(c + 1)
+            finish(c)

@@ -25,6 +25,9 @@ HALF = S // 2
 FIRST_PAIR = (0, 2)
 SECOND_PAIR = (1, 3)
 CHUNKS = (256, 256, 512, 512, 512)
+FIRST_BANKS = 4
+LEAD = 256
+BANKS = 8
 
 
 def tile_list_duty_swap_board_kernel(
@@ -35,7 +38,7 @@ def tile_list_duty_swap_board_kernel(
         lists = ctx.enter_context(tc.tile_pool(name="lists", bufs=1))
         keep = ctx.enter_context(tc.tile_pool(name="keep", bufs=1))
         swap = ctx.enter_context(tc.tile_pool(name="swap", bufs=2))
-        psum = ctx.enter_context(tc.psum_pool(name="psum", bufs=8))
+        psum = ctx.enter_context(tc.psum_pool(name="psum", bufs=1))
 
         l1 = lists.tile([P, S // 16], U16, name="l1")
         l2 = lists.tile([P, S // 16], U16, name="l2")
@@ -53,7 +56,7 @@ def tile_list_duty_swap_board_kernel(
         vb_t = keep.tile([P, PACK], F32, name="vb_t")
         gain_t = keep.tile([P, PACK], F32, name="gain_t")
 
-        nc.vector.memset(planes[:].bitcast(I32), 0)
+        nc.gpsimd.memset(planes[:].bitcast(I32), 0)
         nc.gpsimd.memset(w2s_raw[:].bitcast(I32), 0)
 
         page_rows = page0.rearrange("(p t) c -> t p c", t=PACK)
@@ -76,26 +79,25 @@ def tile_list_duty_swap_board_kernel(
         first = FIRST_PAIR[0]
         nc.sync.dma_start(l1[:], offs)
         load_words(0)
+        load_w1(0)
         for quad in range(4):
-            nc.scalar.dma_start(
+            nc.sync.dma_start(
                 out=planes[32 * quad : 32 * quad + 4 * PASSES, :].bitcast(I32),
                 in_=tab_scales[:, 4 * quad : 4 * quad + 4, :].bitcast(I32),
             )
-        load_w1(0)
-        nc.sync.dma_start(out=w2_raw[:].bitcast(I32), in_=w2_words[0].bitcast(I32))
+        load_words(1)
+        load_w1(1)
         for quad in range(4):
-            nc.scalar.dma_start(
+            nc.sync.dma_start(
                 out=w2s_raw[32 * quad : 32 * quad + 4, :].bitcast(I32),
                 in_=w2_scales[0, 4 * quad : 4 * quad + 4, :].bitcast(I32),
             )
-        load_w1(1)
-        load_words(1)
         load_w1(2)
         load_words(2)
         nc.sync.dma_start(l2[:], offs2)
-        load_wg(first, 0, HALF)
+        load_wg(first, 0, LEAD)
         nc.sync.dma_start(out=page[first][:], in_=page_rows[first])
-        load_wg(first, HALF, S)
+        load_wg(first, LEAD, S)
         nc.sync.dma_start(out=page[FIRST_PAIR[1]][:], in_=page_rows[FIRST_PAIR[1]])
         load_wg(FIRST_PAIR[1], 0, S)
         nc.sync.dma_start(l3[:], offs3)
@@ -103,6 +105,7 @@ def tile_list_duty_swap_board_kernel(
         nc.sync.dma_start(out=va_t[:], in_=va.rearrange("(p t) -> p t", t=PACK))
         nc.sync.dma_start(out=vb_t[:], in_=vb.rearrange("(p t) -> p t", t=PACK))
         nc.sync.dma_start(out=gain_t[:], in_=gain.rearrange("(p t) -> p t", t=PACK))
+        nc.sync.dma_start(out=w2_raw[:].bitcast(I32), in_=w2_words[0].bitcast(I32))
         for t in SECOND_PAIR:
             nc.sync.dma_start(out=page[t][:], in_=page_rows[t])
         for t in reversed(SECOND_PAIR):
@@ -122,7 +125,8 @@ def tile_list_duty_swap_board_kernel(
             if a < PASSES - 1:
                 nc.scalar.copy(out=dst, in_=src)
             else:
-                nc.vector.tensor_copy(out=dst, in_=src)
+                nc.vector.tensor_copy(out=dst[:, 0 : P // 2], in_=src[:, 0 : P // 2])
+                nc.scalar.copy(out=dst[:, P // 2 : P], in_=src[:, P // 2 : P])
 
         def quantize_w1(a):
             nc.vector.quantize_mx(
@@ -135,33 +139,28 @@ def tile_list_duty_swap_board_kernel(
         nc.vector.tensor_copy(picked_planes[:], planes[:].indirect(l1[:]))
         weave_w1(0)
         nc.vector.tensor_copy(
-            out=w2_codes[:].rearrange("p (t m b) -> p t m b", t=PACK, b=2),
-            in_=w2_raw[:].rearrange("p (m t b) -> p t m b", t=PACK, b=2),
-        )
-        nc.vector.tensor_copy(
             out=w2_planes[:].rearrange("p (t m) -> p t m", t=PACK),
             in_=w2s_raw[:].rearrange("p (m t) -> p t m", t=PACK),
         )
         quantize_w1(0)
-        weave_w1(1)
         nc.vector.tensor_copy(picked[1][:], words[1][:].indirect(l1[:]))
+        weave_w1(1)
         quantize_w1(1)
         weave_w1(2)
         quantize_w1(2)
-        for half in range(2):
-            nc.vector.tensor_copy(
-                picked[2][:, half * HALF : (half + 1) * HALF],
-                words[2][:].indirect(l1[:, half * (HALF // 16) : (half + 1) * (HALF // 16)]),
-            )
+        for c0, c1 in ((0, LEAD), (LEAD, HALF), (HALF, S)):
+            nc.vector.tensor_copy(picked[2][:, c0:c1], words[2][:].indirect(l1[:, c0 // 16 : c1 // 16]))
 
         h = [keep.tile([P, S], F32, name="h%d" % t) for t in range(PACK)]
-        groups = [(t, half) for t in FIRST_PAIR + SECOND_PAIR for half in range(2)]
-        sums = {g: psum.tile([P, HALF], F32, name="bank") for g in groups}
-        for a in range(PASSES):
-            for t, half in groups:
-                cols = slice(half * HALF, (half + 1) * HALF)
+        groups = [(first, 0, LEAD), (first, LEAD, HALF), (first, HALF, S)]
+        for t in FIRST_PAIR[1:] + SECOND_PAIR:
+            groups.extend([(t, 0, HALF), (t, HALF, S)])
+        for g, (t, c0, c1) in enumerate(groups):
+            cols = slice(c0, c1)
+            sums = psum.tile([P, HALF], F32, name="bank%d" % (g % FIRST_BANKS))
+            for a in range(PASSES):
                 nc.tensor.matmul_mx(
-                    out=sums[t, half][:],
+                    out=sums[:, 0 : c1 - c0],
                     lhsT=w1_codes[a][:, t * P : (t + 1) * P].bitcast(FP8X4),
                     lhsT_scale=w1_scales[a][:, t * P : (t + 1) * P],
                     rhs=picked[a][:, cols].bitcast(FP8X4),
@@ -169,21 +168,16 @@ def tile_list_duty_swap_board_kernel(
                     start=(a == 0),
                     stop=(a == PASSES - 1),
                 )
-        for t, half in groups:
-            nc.scalar.activation(out=h[t][:, half * HALF : (half + 1) * HALF], in_=sums[t, half][:], func=TANH)
+            nc.scalar.activation(out=h[t][:, cols], in_=sums[:, 0 : c1 - c0], func=TANH)
 
         starts = [sum(CHUNKS[:c]) for c in range(len(CHUNKS))]
         x_bf = [keep.tile([P, w, PACK], BF16, name="x_bf%d" % c, align_bytes=64) for c, w in enumerate(CHUNKS)]
 
         def put(t):
             if t == first:
-                for half in range(2):
-                    cols = slice(half * HALF, (half + 1) * HALF)
+                for c0, c1 in ((0, LEAD), (LEAD, S)):
                     nc.vector.tensor_tensor(
-                        page[t][:].indirect(l2[:, half * (HALF // 16) : (half + 1) * (HALF // 16)]),
-                        h[t][:, cols],
-                        wg[t][:, cols],
-                        MULT,
+                        page[t][:].indirect(l2[:, c0 // 16 : c1 // 16]), h[t][:, c0:c1], wg[t][:, c0:c1], MULT
                     )
             else:
                 nc.vector.tensor_tensor(page[t][:].indirect(l2[:]), h[t][:], wg[t][:], MULT)
@@ -217,6 +211,11 @@ def tile_list_duty_swap_board_kernel(
             for c in range(len(CHUNKS)):
                 round_rows(t, c)
 
+        nc.scalar.copy(
+            out=w2_codes[:].bitcast(U16).rearrange("p (t m) -> p t m", t=PACK),
+            in_=w2_raw[:].bitcast(U16).rearrange("p (m t) -> p t m", t=PACK),
+        )
+
         t0, t1 = SECOND_PAIR
         put(t0)
         put(t1)
@@ -232,11 +231,13 @@ def tile_list_duty_swap_board_kernel(
             round_rows(t0, c)
 
         out_rows = out.rearrange("(p t) c -> p t c", t=PACK)
-        x_codes = [keep.tile([P, w], U32, name="x_codes%d" % c, align_bytes=64) for c, w in enumerate(CHUNKS)]
-        x_scales = [keep.tile([P, w], U8, name="x_scales%d" % c, align_bytes=64) for c, w in enumerate(CHUNKS)]
+        x_codes = {}
+        x_scales = {}
         result = [keep.tile([P, PACK, w], F32, name="result%d" % c) for c, w in enumerate(CHUNKS)]
 
         def quantize_x(c):
+            x_codes[c] = swap.tile([P, CHUNKS[c]], U32, name="x_codes", align_bytes=64)
+            x_scales[c] = swap.tile([P, CHUNKS[c]], U8, name="x_scales", align_bytes=64)
             nc.vector.quantize_mx(
                 out=x_codes[c][:].bitcast(FP8X4), scales=x_scales[c][:], in_=x_bf[c][:].rearrange("p w i -> p (w i)")
             )
@@ -245,7 +246,7 @@ def tile_list_duty_swap_board_kernel(
             w = CHUNKS[c]
             cols = slice(starts[c], starts[c] + w)
             for t in range(PACK):
-                acc = psum.tile([P, HALF], F32, name="bank")
+                acc = psum.tile([P, HALF], F32, name="bank%d" % ((PACK * c + t) % BANKS))
                 nc.tensor.matmul_mx(
                     out=acc[:, 0:w],
                     lhsT=w2_codes[:, 2 * t * P : 2 * (t + 1) * P].bitcast(FP4X4),
@@ -256,7 +257,9 @@ def tile_list_duty_swap_board_kernel(
                     stop=True,
                 )
                 nc.vector.tensor_tensor(result[c][:, t, :], acc[:, 0:w], page[t][:, cols], ADD)
-                if t % 2 == 1:
+                if c == len(CHUNKS) - 1:
+                    nc.sync.dma_start(out=out_rows[:, t, cols], in_=result[c][:, t, :])
+                elif t % 2 == 1:
                     nc.sync.dma_start(out=out_rows[:, t - 1 : t + 1, cols], in_=result[c][:, t - 1 : t + 1, :])
 
         nc.vector.tensor_scalar(

@@ -27,6 +27,7 @@ SECOND_PAIR = (1, 3)
 CHUNKS = (256, 256, 512, 512, 512)
 FIRST_BANKS = 4
 LEAD = 256
+VECTOR_CHUNKS = 2
 BANKS = 8
 
 
@@ -56,8 +57,8 @@ def tile_list_duty_swap_board_kernel(
         vb_t = keep.tile([P, PACK], F32, name="vb_t")
         gain_t = keep.tile([P, PACK], F32, name="gain_t")
 
-        nc.gpsimd.memset(planes[:].bitcast(I32), 0)
-        nc.gpsimd.memset(w2s_raw[:].bitcast(I32), 0)
+        nc.vector.memset(planes[:].bitcast(I32), 0)
+        nc.vector.memset(w2s_raw[:].bitcast(I32), 0)
 
         page_rows = page0.rearrange("(p t) c -> t p c", t=PACK)
         wgs_rows = wgs.rearrange("(q t) s -> t q s", t=PACK)
@@ -85,8 +86,8 @@ def tile_list_duty_swap_board_kernel(
                 out=planes[32 * quad : 32 * quad + 4 * PASSES, :].bitcast(I32),
                 in_=tab_scales[:, 4 * quad : 4 * quad + 4, :].bitcast(I32),
             )
-        load_words(1)
         load_w1(1)
+        load_words(1)
         for quad in range(4):
             nc.sync.dma_start(
                 out=w2s_raw[32 * quad : 32 * quad + 4, :].bitcast(I32),
@@ -143,8 +144,8 @@ def tile_list_duty_swap_board_kernel(
             in_=w2s_raw[:].rearrange("p (m t) -> p t m", t=PACK),
         )
         quantize_w1(0)
-        nc.vector.tensor_copy(picked[1][:], words[1][:].indirect(l1[:]))
         weave_w1(1)
+        nc.vector.tensor_copy(picked[1][:], words[1][:].indirect(l1[:]))
         quantize_w1(1)
         weave_w1(2)
         quantize_w1(2)
@@ -262,14 +263,15 @@ def tile_list_duty_swap_board_kernel(
                 elif t % 2 == 1:
                     nc.sync.dma_start(out=out_rows[:, t - 1 : t + 1, cols], in_=result[c][:, t - 1 : t + 1, :])
 
-        nc.vector.tensor_scalar(
-            out=x_bf[0][:, :, t1],
-            in0=page[t1][:, 0 : CHUNKS[0]],
-            scalar1=gain_t[:, t1 : t1 + 1],
-            scalar2=None,
-            op0=MULT,
-        )
-        for c in range(1, len(CHUNKS)):
+        for c in range(VECTOR_CHUNKS):
+            nc.vector.tensor_scalar(
+                out=x_bf[c][:, :, t1],
+                in0=page[t1][:, starts[c] : starts[c] + CHUNKS[c]],
+                scalar1=gain_t[:, t1 : t1 + 1],
+                scalar2=None,
+                op0=MULT,
+            )
+        for c in range(VECTOR_CHUNKS, len(CHUNKS)):
             round_rows(t1, c)
         quantize_x(0)
         for c in range(len(CHUNKS)):

@@ -100,8 +100,9 @@ def tile_list_duty_swap_board_kernel(
         nc.sync.dma_start(out=page[first][:], in_=page_rows[first])
         load_wg(first, LEAD, S)
         nc.sync.dma_start(out=page[FIRST_PAIR[1]][:], in_=page_rows[FIRST_PAIR[1]])
-        load_wg(FIRST_PAIR[1], 0, S)
+        load_wg(FIRST_PAIR[1], 0, HALF)
         nc.sync.dma_start(l3[:], offs3)
+        load_wg(FIRST_PAIR[1], HALF, S)
         nc.sync.dma_start(l4[:], offs4)
         nc.sync.dma_start(out=va_t[:], in_=va.rearrange("(p t) -> p t", t=PACK))
         nc.sync.dma_start(out=vb_t[:], in_=vb.rearrange("(p t) -> p t", t=PACK))
@@ -174,14 +175,10 @@ def tile_list_duty_swap_board_kernel(
         starts = [sum(CHUNKS[:c]) for c in range(len(CHUNKS))]
         x_bf = [keep.tile([P, w, PACK], BF16, name="x_bf%d" % c, align_bytes=64) for c, w in enumerate(CHUNKS)]
 
-        def put(t):
-            if t == first:
-                for c0, c1 in ((0, LEAD), (LEAD, S)):
-                    nc.vector.tensor_tensor(
-                        page[t][:].indirect(l2[:, c0 // 16 : c1 // 16]), h[t][:, c0:c1], wg[t][:, c0:c1], MULT
-                    )
-            else:
-                nc.vector.tensor_tensor(page[t][:].indirect(l2[:]), h[t][:], wg[t][:], MULT)
+        def put(t, c0, c1):
+            nc.vector.tensor_tensor(
+                page[t][:].indirect(l2[:, c0 // 16 : c1 // 16]), h[t][:, c0:c1], wg[t][:, c0:c1], MULT
+            )
 
         def fetch(t, offsets, factor, tag):
             side = swap.tile([P, PAIRS], F32, name="side_" + tag)
@@ -198,11 +195,13 @@ def tile_list_duty_swap_board_kernel(
             nc.scalar.activation(out=x_bf[c][:, :, t], in_=page[t][:, cols], func=COPY, scale=gain_t[:, t : t + 1])
 
         t0, t1 = FIRST_PAIR
-        put(t0)
-        put(t1)
+        put(t0, 0, LEAD)
+        put(t0, LEAD, S)
+        put(t1, 0, HALF)
         a0, va0 = fetch(t0, l3, va_t, "a")
-        a1, va1 = fetch(t1, l3, va_t, "a")
+        put(t1, HALF, S)
         b0, vb0 = fetch(t0, l4, vb_t, "b")
+        a1, va1 = fetch(t1, l3, va_t, "a")
         b1, vb1 = fetch(t1, l4, vb_t, "b")
         put_back(t0, l3, va0, b0)
         put_back(t1, l3, va1, b1)
@@ -218,8 +217,8 @@ def tile_list_duty_swap_board_kernel(
         )
 
         t0, t1 = SECOND_PAIR
-        put(t0)
-        put(t1)
+        put(t0, 0, S)
+        put(t1, 0, S)
         a0, va0 = fetch(t0, l3, va_t, "a")
         b0, vb0 = fetch(t0, l4, vb_t, "b")
         a1, va1 = fetch(t1, l3, va_t, "a")

from contextlib import ExitStack

import concourse.mybir as mybir

K, T, S, H, T2, PAIRS = 1536, 2048, 1024, 512, 2048, 512
FLOPS = 2 * K * H * S + 2 * H * H * T2

F32 = mybir.dt.float32
BF16 = mybir.dt.bfloat16
I32 = mybir.dt.int32
U32 = mybir.dt.uint32
U16 = mybir.dt.uint16
U8 = mybir.dt.uint8
FP8X4 = mybir.dt.float8_e4m3fn_x4
FP4X4 = mybir.dt.float4_e2m1fn_x4
MULT = mybir.AluOpType.mult
ADD = mybir.AluOpType.add
COPY = mybir.ActivationFunctionType.Copy
TANH = mybir.ActivationFunctionType.Tanh

P = 128
PACK = 4
PASSES = K // (P * PACK)
HALF = S // 2
FIRST_PAIR = (0, 2)
SECOND_PAIR = (1, 3)
CHUNKS = (256, 256, 512, 512, 512)
FIRST_BANKS = 4
LEAD = 256
VECTOR_CHUNKS = 2
BANKS = 8


def tile_list_duty_swap_board_kernel(
    tc, tab_words, tab_scales, offs, w1, page0, wgs, offs2, offs3, offs4, va, vb, gain, w2_words, w2_scales, out
):
    nc = tc.nc
    with ExitStack() as ctx:
        lists = ctx.enter_context(tc.tile_pool(name="lists", bufs=1))
        keep = ctx.enter_context(tc.tile_pool(name="keep", bufs=1))
        swap = ctx.enter_context(tc.tile_pool(name="swap", bufs=2))
        psum = ctx.enter_context(tc.psum_pool(name="psum", bufs=1))

        l1 = lists.tile([P, S // 16], U16, name="l1")
        l2 = lists.tile([P, S // 16], U16, name="l2")
        l3 = lists.tile([P, PAIRS // 16], U16, name="l3")
        l4 = lists.tile([P, PAIRS // 16], U16, name="l4")

        words = [keep.tile([P, T], U32, name="words%d" % a, align_bytes=64) for a in range(PASSES)]
        planes = keep.tile([P, T], U8, name="planes", align_bytes=64)
        w1_raw = [keep.tile([P, PACK, H], F32, name="w1_raw%d" % a) for a in range(PASSES)]
        page = [keep.tile([P, T2], F32, name="page%d" % t, align_bytes=64) for t in range(PACK)]
        wg = [keep.tile([P, S], F32, name="wg%d" % t) for t in range(PACK)]
        w2_raw = keep.tile([P, 2 * H], U8, name="w2_raw", align_bytes=64)
        w2s_raw = keep.tile([P, H], U8, name="w2s_raw", align_bytes=64)
        va_t = keep.tile([P, PACK], F32, name="va_t")
        vb_t = keep.tile([P, PACK], F32, name="vb_t")
        gain_t = keep.tile([P, PACK], F32, name="gain_t")

        nc.vector.memset(planes[:].bitcast(I32), 0)
        nc.vector.memset(w2s_raw[:].bitcast(I32), 0)

        page_rows = page0.rearrange("(p t) c -> t p c", t=PACK)
        wgs_rows = wgs.rearrange("(q t) s -> t q s", t=PACK)

        def load_words(a):
            nc.sync.dma_start(
                out=words[a][:].bitcast(I32), in_=tab_words[a].rearrange("p n i -> p (n i)").bitcast(I32)
            )

        def load_w1(a):
            nc.sync.dma_start(
                out=w1_raw[a][:], in_=w1[512 * a : 512 * (a + 1), :].rearrange("(p j) c -> p j c", j=PACK)
            )

        def load_wg(t, c0, c1):
            for quad in (0, 2, 1, 3):
                nc.sync.dma_start(out=wg[t][32 * quad : 32 * quad + 32, c0:c1], in_=wgs_rows[t][:, c0:c1])

        first = FIRST_PAIR[0]
        nc.sync.dma_start(l1[:], offs)
        load_words(0)
        load_w1(0)
        for quad in range(4):
            nc.sync.dma_start(
                out=planes[32 * quad : 32 * quad + 4 * PASSES, :].bitcast(I32),
                in_=tab_scales[:, 4 * quad : 4 * quad + 4, :].bitcast(I32),
            )
        load_w1(1)
        load_words(1)
        for quad in range(4):
            nc.sync.dma_start(
                out=w2s_raw[32 * quad : 32 * quad + 4, :].bitcast(I32),
                in_=w2_scales[0, 4 * quad : 4 * quad + 4, :].bitcast(I32),
            )
        load_w1(2)
        load_words(2)
        nc.sync.dma_start(l2[:], offs2)
        load_wg(first, 0, LEAD)
        nc.sync.dma_start(out=page[first][:], in_=page_rows[first])
        load_wg(first, LEAD, S)
        nc.sync.dma_start(out=page[FIRST_PAIR[1]][:], in_=page_rows[FIRST_PAIR[1]])
        load_wg(FIRST_PAIR[1], 0, HALF)
        nc.sync.dma_start(l3[:], offs3)
        load_wg(FIRST_PAIR[1], HALF, S)
        nc.sync.dma_start(l4[:], offs4)
        nc.sync.dma_start(out=va_t[:], in_=va.rearrange("(p t) -> p t", t=PACK))
        nc.sync.dma_start(out=vb_t[:], in_=vb.rearrange("(p t) -> p t", t=PACK))
        nc.sync.dma_start(out=gain_t[:], in_=gain.rearrange("(p t) -> p t", t=PACK))
        nc.sync.dma_start(out=w2_raw[:].bitcast(I32), in_=w2_words[0].bitcast(I32))
        for t in SECOND_PAIR:
            nc.sync.dma_start(out=page[t][:], in_=page_rows[t])
        for t in reversed(SECOND_PAIR):
            load_wg(t, 0, S)

        picked = [keep.tile([P, S], U32, name="picked%d" % a, align_bytes=64) for a in range(PASSES)]
        picked_planes = keep.tile([P, S], U8, name="picked_planes", align_bytes=64)
        w1_bf = [keep.tile([P, PACK, P, PACK], BF16, name="w1_bf%d" % a, align_bytes=64) for a in range(PASSES)]
        w1_codes = [keep.tile([P, H], U32, name="w1_codes%d" % a, align_bytes=64) for a in range(PASSES)]
        w1_scales = [keep.tile([P, H], U8, name="w1_scales%d" % a, align_bytes=64) for a in range(PASSES)]
        w2_codes = keep.tile([P, 2 * H], U8, name="w2_codes", align_bytes=64)
        w2_planes = keep.tile([P, H], U8, name="w2_planes", align_bytes=64)

        def weave_w1(a):
            dst = w1_bf[a][:].rearrange("p t m j -> p m t j")
            src = w1_raw[a][:].rearrange("p j (m t) -> p m t j", t=PACK)
            if a < PASSES - 1:
                nc.scalar.copy(out=dst, in_=src)
            else:
                nc.vector.tensor_copy(out=dst[:, 0 : P // 2], in_=src[:, 0 : P // 2])
                nc.scalar.copy(out=dst[:, P // 2 : P], in_=src[:, P // 2 : P])

        def quantize_w1(a):
            nc.vector.quantize_mx(
                out=w1_codes[a][:].bitcast(FP8X4),
                scales=w1_scales[a][:],
                in_=w1_bf[a][:].rearrange("p t m j -> p (t m j)"),
            )

        nc.vector.tensor_copy(picked[0][:], words[0][:].indirect(l1[:]))
        nc.vector.tensor_copy(picked_planes[:], planes[:].indirect(l1[:]))
        weave_w1(0)
        nc.vector.tensor_copy(
            out=w2_planes[:].rearrange("p (t m) -> p t m", t=PACK),
            in_=w2s_raw[:].rearrange("p (m t) -> p t m", t=PACK),
        )
        quantize_w1(0)
        weave_w1(1)
        nc.vector.tensor_copy(picked[1][:], words[1][:].indirect(l1[:]))
        quantize_w1(1)
        weave_w1(2)
        quantize_w1(2)
        for c0, c1 in ((0, LEAD), (LEAD, HALF), (HALF, S)):
            nc.vector.tensor_copy(picked[2][:, c0:c1], words[2][:].indirect(l1[:, c0 // 16 : c1 // 16]))

        h = [keep.tile([P, S], F32, name="h%d" % t) for t in range(PACK)]
        groups = [(first, 0, LEAD), (first, LEAD, HALF), (first, HALF, S)]
        for t in FIRST_PAIR[1:] + SECOND_PAIR:
            groups.extend([(t, 0, HALF), (t, HALF, S)])
        for g, (t, c0, c1) in enumerate(groups):
            cols = slice(c0, c1)
            sums = psum.tile([P, HALF], F32, name="bank%d" % (g % FIRST_BANKS))
            for a in range(PASSES):
                nc.tensor.matmul_mx(
                    out=sums[:, 0 : c1 - c0],
                    lhsT=w1_codes[a][:, t * P : (t + 1) * P].bitcast(FP8X4),
                    lhsT_scale=w1_scales[a][:, t * P : (t + 1) * P],
                    rhs=picked[a][:, cols].bitcast(FP8X4),
                    rhs_scale=picked_planes[4 * a : P, cols],
                    start=(a == 0),
                    stop=(a == PASSES - 1),
                )
            nc.scalar.activation(out=h[t][:, cols], in_=sums[:, 0 : c1 - c0], func=TANH)

        starts = [sum(CHUNKS[:c]) for c in range(len(CHUNKS))]
        x_bf = [keep.tile([P, w, PACK], BF16, name="x_bf%d" % c, align_bytes=64) for c, w in enumerate(CHUNKS)]

        def put(t, c0, c1):
            nc.vector.tensor_tensor(
                page[t][:].indirect(l2[:, c0 // 16 : c1 // 16]), h[t][:, c0:c1], wg[t][:, c0:c1], MULT
            )

        def fetch(t, offsets, factor, tag):
            side = swap.tile([P, PAIRS], F32, name="side_" + tag)
            scaled = swap.tile([P, PAIRS], F32, name="scaled_" + tag)
            nc.vector.tensor_copy(side[:], page[t][:].indirect(offsets[:]))
            nc.scalar.activation(out=scaled[:], in_=side[:], func=COPY, scale=factor[:, t : t + 1])
            return side, scaled

        def put_back(t, offsets, scaled, other):
            nc.vector.tensor_tensor(page[t][:].indirect(offsets[:]), scaled[:], other[:], ADD)

        def round_rows(t, c):
            cols = slice(starts[c], starts[c] + CHUNKS[c])
            nc.scalar.activation(out=x_bf[c][:, :, t], in_=page[t][:, cols], func=COPY, scale=gain_t[:, t : t + 1])

        t0, t1 = FIRST_PAIR
        put(t0, 0, LEAD)
        put(t0, LEAD, S)
        put(t1, 0, HALF)
        a0, va0 = fetch(t0, l3, va_t, "a")
        put(t1, HALF, S)
        b0, vb0 = fetch(t0, l4, vb_t, "b")
        a1, va1 = fetch(t1, l3, va_t, "a")
        b1, vb1 = fetch(t1, l4, vb_t, "b")
        put_back(t0, l3, va0, b0)
        put_back(t1, l3, va1, b1)
        put_back(t0, l4, vb0, a0)
        put_back(t1, l4, vb1, a1)
        for t in FIRST_PAIR:
            for c in range(len(CHUNKS)):
                round_rows(t, c)

        nc.scalar.copy(
            out=w2_codes[:].bitcast(U16).rearrange("p (t m) -> p t m", t=PACK),
            in_=w2_raw[:].bitcast(U16).rearrange("p (m t) -> p t m", t=PACK),
        )

        t0, t1 = SECOND_PAIR
        put(t0, 0, S)
        put(t1, 0, S)
        a0, va0 = fetch(t0, l3, va_t, "a")
        b0, vb0 = fetch(t0, l4, vb_t, "b")
        a1, va1 = fetch(t1, l3, va_t, "a")
        put_back(t0, l3, va0, b0)
        b1, vb1 = fetch(t1, l4, vb_t, "b")
        put_back(t0, l4, vb0, a0)
        put_back(t1, l3, va1, b1)
        put_back(t1, l4, vb1, a1)
        for c in range(len(CHUNKS)):
            round_rows(t0, c)

        out_rows = out.rearrange("(p t) c -> p t c", t=PACK)
        x_codes = {}
        x_scales = {}
        result = [keep.tile([P, PACK, w], F32, name="result%d" % c) for c, w in enumerate(CHUNKS)]

        def quantize_x(c):
            x_codes[c] = swap.tile([P, CHUNKS[c]], U32, name="x_codes", align_bytes=64)
            x_scales[c] = swap.tile([P, CHUNKS[c]], U8, name="x_scales", align_bytes=64)
            nc.vector.quantize_mx(
                out=x_codes[c][:].bitcast(FP8X4), scales=x_scales[c][:], in_=x_bf[c][:].rearrange("p w i -> p (w i)")
            )

        def finish(c):
            w = CHUNKS[c]
            cols = slice(starts[c], starts[c] + w)
            for t in range(PACK):
                acc = psum.tile([P, HALF], F32, name="bank%d" % ((PACK * c + t) % BANKS))
                nc.tensor.matmul_mx(
                    out=acc[:, 0:w],
                    lhsT=w2_codes[:, 2 * t * P : 2 * (t + 1) * P].bitcast(FP4X4),
                    lhsT_scale=w2_planes[:, t * P : (t + 1) * P],
                    rhs=x_codes[c][:].bitcast(FP8X4),
                    rhs_scale=x_scales[c][:],
                    start=True,
                    stop=True,
                )
                nc.vector.tensor_tensor(result[c][:, t, :], acc[:, 0:w], page[t][:, cols], ADD)
                if c == len(CHUNKS) - 1:
                    nc.sync.dma_start(out=out_rows[:, t, cols], in_=result[c][:, t, :])
                elif t % 2 == 1:
                    nc.sync.dma_start(out=out_rows[:, t - 1 : t + 1, cols], in_=result[c][:, t - 1 : t + 1, :])

        for c in range(VECTOR_CHUNKS):
            nc.vector.tensor_scalar(
                out=x_bf[c][:, :, t1],
                in0=page[t1][:, starts[c] : starts[c] + CHUNKS[c]],
                scalar1=gain_t[:, t1 : t1 + 1],
                scalar2=None,
                op0=MULT,
            )
        for c in range(VECTOR_CHUNKS, len(CHUNKS)):
            round_rows(t1, c)
        quantize_x(0)
        for c in range(len(CHUNKS)):
            if c + 1 < len(CHUNKS):
                quantize_x(c + 1)
            finish(c)
